import numpy as np
import ml_dtypes


def mxq(x, axis, fmt="e4m3"):
    dtype, down = {"e4m3": (ml_dtypes.float8_e4m3fn, 7), "e5m2": (ml_dtypes.float8_e5m2, 14)}[fmt]
    v = np.moveaxis(np.asarray(x, np.float32).astype(ml_dtypes.bfloat16).astype(np.float64), axis, -1)
    blocks = v.reshape(v.shape[:-1] + (-1, 32))
    amax = np.abs(blocks).max(-1, keepdims=True)
    byte = np.maximum(np.where(amax > 0, np.frexp(amax)[1] - 1 + 127, 0) - down, 1)
    scale = np.exp2(byte - 127.0)
    codes = (blocks / scale).astype(np.float32).astype(dtype).astype(np.float64)
    return np.moveaxis((codes * scale).reshape(v.shape), -1, axis)


WIDE = False


def mx_kscale(k):
    if not WIDE:
        return np.ones(k)
    levels = np.array([30, -30])
    if k % 512:
        return np.exp2(np.random.permutation(np.resize(levels, k // 32))).repeat(32)
    a = np.empty((k // 512, 16))
    for p in range(k // 512):
        a[p, :8] = np.random.permutation(np.resize(levels, 8))
        for g in range(8):
            far = levels[np.abs(levels - a[p, g]) >= 10]
            a[p, g + 8] = far[np.random.randint(len(far))]
    return np.exp2(a.ravel()).repeat(32)


def f64(x):
    return np.asarray(x).astype(np.float64)


def striped(idx):
    return np.tile(np.asarray(idx).reshape(-1, 16).T, (8, 1)).astype(np.uint16)


def unstriped(offs):
    return offs[:16].T.reshape(-1).astype(np.int64)


def striped8(idx):
    return np.asarray(idx).reshape(8, -1, 16).transpose(0, 2, 1).reshape(128, -1).astype(np.uint16)


def unstriped8(offs):
    return offs.reshape(8, 16, -1).transpose(0, 2, 1).reshape(8, -1).astype(np.int64)


def pick8(x, idx, run):
    r = np.arange(len(x))
    return x[r[:, None], idx[r % (8 * run) // run]]


def bf(x):
    return np.asarray(x, np.float32).astype(ml_dtypes.bfloat16)


def planes(Y):
    r, m = Y.shape
    b = f64(bf(Y)).reshape(r // 32, 32, m)
    amax = np.abs(b).max(1)
    byte = np.clip(np.where(amax > 0, np.frexp(amax)[1] - 1 + 127 - 7, 1), 1, 254)
    codes = (b * np.exp2(127.0 - byte)[:, None, :]).reshape(r, m).astype(np.float32).astype(ml_dtypes.float8_e4m3fn).view(np.uint8)
    words = codes.reshape(r // 512, 128, 4, m).transpose(0, 1, 3, 2)
    return np.ascontiguousarray(words), np.ascontiguousarray(byte.astype(np.uint8).reshape(r // 512, 16, m))


K, N, T, J = 512, 512, 1024, 512


def setup_inputs():
    n = np.random.standard_normal
    idx = np.stack([np.random.permutation(T)[:J] for _ in range(8)])
    idx2 = np.random.permutation(T)[:J]
    fj = mx_kscale(J)
    return {
        "xf": (n((K, T))).astype(np.float32),
        "g": (n((N, T)) * np.exp(0.5 * n((1, T)))).astype(np.float32),
        "ra": (np.random.uniform(0.5, 1.5, (1, J)) * fj).astype(np.float32),
        "rb": (np.random.uniform(0.5, 1.5, (1, J)) / fj).astype(np.float32),
        "offs": striped8(idx),
        "offs2": striped(idx2),
    }


def reference(xf, g, ra, rb, offs, offs2):
    idx = unstriped8(offs)
    idx2 = unstriped(offs2)
    xs = pick8(f64(xf), idx, 64) * f64(ra)
    xj = xs.T
    gs = f64(g)[:, idx2] * f64(rb)
    gj = gs.T
    xjq = mxq(xj, 0, "e4m3")
    gjq = mxq(gj, 0, "e5m2")
    w = xjq.T @ gjq
    y = 0.04 * w
    words, scales = planes(y)
    return y, words, scales

@@ -1,0 +1,123 @@
+from contextlib import ExitStack
+
+import concourse.mybir as mybir
+from concourse.masks import make_identity
+
+K, N, T, J = 512, 512, 1024, 512
+FLOPS = 2 * K * N * J
+
+F32 = mybir.dt.float32
+BF16 = mybir.dt.bfloat16
+I32 = mybir.dt.int32
+U32 = mybir.dt.uint32
+U16 = mybir.dt.uint16
+U8 = mybir.dt.uint8
+E4M3 = mybir.dt.float8_e4m3fn_x4
+E5M2 = mybir.dt.float8_e5m2_x4
+MULT = mybir.AluOpType.mult
+COPY = mybir.ActivationFunctionType.Copy
+
+P = 128
+PACK = 4
+OUT_SCALE = 0.04
+
+
+def tile_moe_expert_heads_wgrad_pl_kernel(tc, xf, g, ra, rb, offs, offs2, out_0, out_1, out_2):
+    nc = tc.nc
+    with ExitStack() as ctx:
+        keep = ctx.enter_context(tc.tile_pool(name="keep", bufs=1))
+        ring = ctx.enter_context(tc.tile_pool(name="ring", bufs=3))
+        turn = ctx.enter_context(tc.psum_pool(name="turn", bufs=4))
+        sums = ctx.enter_context(tc.psum_pool(name="sums", bufs=4))
+
+        x_list = keep.tile([P, J // 16], U16, name="x_list")
+        g_list = keep.tile([P, J // 16], U16, name="g_list")
+        ra_col = keep.tile([P, PACK], F32, name="ra_col")
+        rb_col = keep.tile([P, PACK], F32, name="rb_col")
+        g_win = [keep.tile([P, T], F32, name="g_win%d" % u) for u in range(PACK)]
+        x_win = [keep.tile([P, T], F32, name="x_win%d" % t) for t in range(PACK)]
+        x_rows = xf.rearrange("(p t) c -> t p c", t=PACK)
+
+        nc.scalar.dma_start(rb_col[:], rb[0].rearrange("(p c) -> p c", c=PACK))
+        nc.sync.dma_start(g_list[:], offs2)
+        nc.sync.dma_start(g_win[0][:], g[0:P, :])
+        nc.scalar.dma_start(ra_col[:], ra[0].rearrange("(p c) -> p c", c=PACK))
+        nc.sync.dma_start(g_win[1][:], g[P : 2 * P, :])
+        nc.sync.dma_start(x_list[:], offs)
+        for u in range(2, PACK):
+            nc.sync.dma_start(g_win[u][:], g[u * P : (u + 1) * P, :])
+        for t in range(PACK):
+            nc.sync.dma_start(x_win[t][:], x_rows[t])
+
+        ident = keep.tile([P, P], F32, name="ident")
+        make_identity(nc, ident[:])
+
+        def spread(col, copy, name):
+            bank = turn.tile([P, PACK, P], F32, name="bank")
+            for c in range(PACK):
+                nc.tensor.transpose(bank[:, c, :], col[:, c : c + 1].to_broadcast([P, P]), ident[:])
+            row = keep.tile([P, J], F32, name=name)
+            copy(row[:].rearrange("q (p c) -> q p c", c=PACK), bank[:].rearrange("q c p -> q p c"))
+            return row
+
+        rb_row = spread(rb_col, nc.vector.tensor_copy, "rb_row")
+        ra_row = spread(ra_col, nc.scalar.copy, "ra_row")
+
+        def gather_and_turn(window, offsets, weights, grouped):
+            picked = ring.tile([P, J], F32, name="picked")
+            nc.vector.tensor_tensor(picked[:], window[:].indirect(offsets[:]), weights[:], MULT)
+            pairs = ring.tile([P, J], BF16, name="pairs")
+            nc.scalar.copy(
+                pairs[:].rearrange("q (u p e) -> q u p e", u=2, e=2),
+                picked[:].rearrange("q (p u e) -> q u p e", u=2, e=2),
+            )
+            words = pairs[:].bitcast(F32)
+            bank = turn.tile([P, 2, P], F32, name="bank")
+            for u in range(2):
+                nc.tensor.transpose(bank[:, u, :], words[:, u * P : (u + 1) * P], ident[:])
+            nc.scalar.copy(
+                grouped.bitcast(F32).rearrange("p (m u) -> p m u", u=2),
+                bank[:].rearrange("p u m -> p m u"),
+            )
+
+        g_grouped = keep.tile([P, N * PACK], BF16, name="g_grouped", align_bytes=64)
+        for u in range(PACK):
+            gather_and_turn(g_win[u], g_list, rb_row, g_grouped[:, u * P * PACK : (u + 1) * P * PACK])
+        g_codes = keep.tile([P, N], U32, name="g_codes", align_bytes=64)
+        g_scales = keep.tile([P, N], U8, name="g_scales", align_bytes=64)
+        nc.vector.quantize_mx(g_codes[:].bitcast(E5M2), g_scales[:], g_grouped[:])
+
+        y = keep.tile([P, PACK, N], F32, name="y")
+        y_rows = out_0.rearrange("(p t) n -> t p n", t=PACK)
+        for t in range(PACK):
+            x_grouped = keep.tile([P, P * PACK], BF16, name="x_grouped%d" % t, align_bytes=64)
+            gather_and_turn(x_win[t], x_list, ra_row, x_grouped[:])
+            x_codes = keep.tile([P, P], U32, name="x_codes%d" % t, align_bytes=64)
+            x_scales = keep.tile([P, P], U8, name="x_scales%d" % t, align_bytes=64)
+            nc.vector.quantize_mx(x_codes[:].bitcast(E4M3), x_scales[:], x_grouped[:])
+            acc = sums.tile([P, N], F32, name="acc")
+            nc.tensor.matmul_mx(
+                acc[:],
+                lhsT=x_codes[:].bitcast(E4M3),
+                lhsT_scale=x_scales[:],
+                rhs=g_codes[:].bitcast(E5M2),
+                rhs_scale=g_scales[:],
+                start=True,
+                stop=True,
+            )
+            nc.scalar.activation(y[:, t, :], acc[:], COPY, scale=OUT_SCALE)
+            nc.sync.dma_start(y_rows[t], y[:, t, :])
+
+        y_grouped = keep.tile([P, N, PACK], BF16, name="y_grouped", align_bytes=64)
+        y_codes = keep.tile([P, N], U32, name="y_codes", align_bytes=64)
+        y_scales = keep.tile([P, N], U8, name="y_scales", align_bytes=64)
+        nc.vector.tensor_copy(
+            y_grouped[:].rearrange("p (c i) t -> p c t i", i=4),
+            y[:].rearrange("p t (c i) -> p c t i", i=4),
+        )
+        nc.vector.quantize_mx(y_codes[:].bitcast(E4M3), y_scales[:], y_grouped[:].rearrange("p n t -> p (n t)"))
+        nc.sync.dma_start(out_1[0].rearrange("p n t -> p (n t)").bitcast(I32), y_codes[:].bitcast(I32))
+        scale_rows = out_2[0].bitcast(I32)
+        for q in range(4):
+            queue = nc.sync if q % 2 else nc.scalar
+            queue.dma_start(scale_rows[4 * q : 4 * q + 4, :], y_scales[32 * q : 32 * q + 4, :].bitcast(I32))

@@ -19,6 +19,8 @@ COPY = mybir.ActivationFunctionType.Copy
 
 P = 128
 PACK = 4
+TILES = 2 * PACK
+HALF = J // 2
 OUT_SCALE = 0.04
 
 
@@ -27,97 +29,146 @@ def tile_moe_expert_heads_wgrad_pl_kernel(tc, xf, g, ra, rb, offs, offs2, out_0,
     with ExitStack() as ctx:
         keep = ctx.enter_context(tc.tile_pool(name="keep", bufs=1))
         ring = ctx.enter_context(tc.tile_pool(name="ring", bufs=3))
-        turn = ctx.enter_context(tc.psum_pool(name="turn", bufs=4))
-        sums = ctx.enter_context(tc.psum_pool(name="sums", bufs=4))
+        psum = ctx.enter_context(tc.psum_pool(name="psum", bufs=1))
 
         x_list = keep.tile([P, J // 16], U16, name="x_list")
         g_list = keep.tile([P, J // 16], U16, name="g_list")
-        ra_col = keep.tile([P, PACK], F32, name="ra_col")
-        rb_col = keep.tile([P, PACK], F32, name="rb_col")
-        g_win = [keep.tile([P, T], F32, name="g_win%d" % u) for u in range(PACK)]
-        x_win = [keep.tile([P, T], F32, name="x_win%d" % t) for t in range(PACK)]
+        ra_col = keep.tile([P, 2, 2], F32, name="ra_col")
+        rb_col = keep.tile([P, 2, 2], F32, name="rb_col")
+        windows = [keep.tile([P, T], F32, name="window%d" % i, tag="window%d" % i, align_bytes=64) for i in range(TILES)]
         x_rows = xf.rearrange("(p t) c -> t p c", t=PACK)
+        g_rows = g.rearrange("(u p) c -> u p c", p=P)
 
-        nc.scalar.dma_start(rb_col[:], rb[0].rearrange("(p c) -> p c", c=PACK))
+        nc.scalar.dma_start(rb_col[:], rb[0].rearrange("(h p c) -> p h c", h=2, c=2))
         nc.sync.dma_start(g_list[:], offs2)
-        nc.sync.dma_start(g_win[0][:], g[0:P, :])
-        nc.scalar.dma_start(ra_col[:], ra[0].rearrange("(p c) -> p c", c=PACK))
-        nc.sync.dma_start(g_win[1][:], g[P : 2 * P, :])
+        nc.sync.dma_start(windows[0][:], g_rows[0])
+        nc.scalar.dma_start(ra_col[:], ra[0].rearrange("(h p c) -> p h c", h=2, c=2))
+        nc.sync.dma_start(windows[1][:], g_rows[1])
         nc.sync.dma_start(x_list[:], offs)
         for u in range(2, PACK):
-            nc.sync.dma_start(g_win[u][:], g[u * P : (u + 1) * P, :])
+            nc.sync.dma_start(windows[u][:], g_rows[u])
         for t in range(PACK):
-            nc.sync.dma_start(x_win[t][:], x_rows[t])
+            nc.sync.dma_start(windows[PACK + t][:], x_rows[t])
 
         ident = keep.tile([P, P], F32, name="ident")
         make_identity(nc, ident[:])
 
-        def spread(col, copy, name):
-            bank = turn.tile([P, PACK, P], F32, name="bank")
-            for c in range(PACK):
-                nc.tensor.transpose(bank[:, c, :], col[:, c : c + 1].to_broadcast([P, P]), ident[:])
+        def spread(col, name, first_bank):
             row = keep.tile([P, J], F32, name=name)
-            copy(row[:].rearrange("q (p c) -> q p c", c=PACK), bank[:].rearrange("q c p -> q p c"))
+            for h in range(2):
+                bank = psum.tile([P, 2, P], F32, name="%s_bank%d" % (name, h), tag="bank%d" % (first_bank + h))
+                for c in range(2):
+                    nc.tensor.transpose(bank[:, c, :], col[:, h, c : c + 1].to_broadcast([P, P]), ident[:])
+                nc.scalar.copy(
+                    row[:, h * HALF : (h + 1) * HALF].rearrange("q (p c) -> q p c", c=2),
+                    bank[:].rearrange("q c p -> q p c"),
+                )
             return row
 
-        rb_row = spread(rb_col, nc.vector.tensor_copy, "rb_row")
-        ra_row = spread(ra_col, nc.scalar.copy, "ra_row")
+        rb_row = spread(rb_col, "rb_row", 0)
+        ra_row = spread(ra_col, "ra_row", 2)
 
-        def gather_and_turn(window, offsets, weights, grouped):
-            picked = ring.tile([P, J], F32, name="picked")
-            nc.vector.tensor_tensor(picked[:], window[:].indirect(offsets[:]), weights[:], MULT)
-            pairs = ring.tile([P, J], BF16, name="pairs")
-            nc.scalar.copy(
-                pairs[:].rearrange("q (u p e) -> q u p e", u=2, e=2),
-                picked[:].rearrange("q (p u e) -> q u p e", u=2, e=2),
-            )
-            words = pairs[:].bitcast(F32)
-            bank = turn.tile([P, 2, P], F32, name="bank")
-            for u in range(2):
-                nc.tensor.transpose(bank[:, u, :], words[:, u * P : (u + 1) * P], ident[:])
-            nc.scalar.copy(
-                grouped.bitcast(F32).rearrange("p (m u) -> p m u", u=2),
-                bank[:].rearrange("p u m -> p m u"),
-            )
-
-        g_grouped = keep.tile([P, N * PACK], BF16, name="g_grouped", align_bytes=64)
-        for u in range(PACK):
-            gather_and_turn(g_win[u], g_list, rb_row, g_grouped[:, u * P * PACK : (u + 1) * P * PACK])
-        g_codes = keep.tile([P, N], U32, name="g_codes", align_bytes=64)
         g_scales = keep.tile([P, N], U8, name="g_scales", align_bytes=64)
-        nc.vector.quantize_mx(g_codes[:].bitcast(E5M2), g_scales[:], g_grouped[:])
-
-        y = keep.tile([P, PACK, N], F32, name="y")
         y_rows = out_0.rearrange("(p t) n -> t p n", t=PACK)
-        for t in range(PACK):
-            x_grouped = keep.tile([P, P * PACK], BF16, name="x_grouped%d" % t, align_bytes=64)
-            gather_and_turn(x_win[t], x_list, ra_row, x_grouped[:])
-            x_codes = keep.tile([P, P], U32, name="x_codes%d" % t, align_bytes=64)
-            x_scales = keep.tile([P, P], U8, name="x_scales%d" % t, align_bytes=64)
-            nc.vector.quantize_mx(x_codes[:].bitcast(E4M3), x_scales[:], x_grouped[:])
-            acc = sums.tile([P, N], F32, name="acc")
+        banks, grouped, sums_of = {}, {}, {}
+
+        def gather_and_turn(i):
+            offsets, weights = (g_list, rb_row) if i < PACK else (x_list, ra_row)
+            pieces = 2 if i in (0, TILES - 1) else 1
+            width = J // pieces
+            pairs = ring.tile([P, 2, P, 2], BF16, name="pairs")
+            for h in range(pieces):
+                slots = slice(h * width, (h + 1) * width)
+                picked = keep.tile([P, width], F32, name="picked%d_%d" % (i, h), tag="stage%d_%d" % (i, h), align_bytes=64)
+                nc.vector.tensor_tensor(
+                    picked[:],
+                    windows[i][:].indirect(offsets[:, h * width // 16 : (h + 1) * width // 16]),
+                    weights[:, slots],
+                    MULT,
+                )
+                nc.scalar.copy(
+                    pairs[:, :, h * width // PACK : (h + 1) * width // PACK, :],
+                    picked[:].rearrange("q (p u e) -> q u p e", u=2, e=2),
+                )
+            words = pairs[:].rearrange("q u p e -> q (u p e)").bitcast(F32)
+            banks[i] = psum.tile([P, 2, P], F32, name="turned%d" % i, tag="bank%d" % (i % 4))
+            for u in range(2):
+                nc.tensor.transpose(banks[i][:, u, :], words[:, u * P : (u + 1) * P], ident[:])
+
+        def regroup(i, y_flat=None):
+            if i == TILES - 1:
+                grouped[i] = y_flat[:, 2 * N - P : 2 * N + P].bitcast(BF16)
+            else:
+                tag = "stage%d_0" % (i + 1)
+                grouped[i] = keep.tile([P, J], BF16, name="grouped%d" % i, tag=tag, align_bytes=64)[:]
+            nc.scalar.copy(
+                grouped[i].bitcast(F32).rearrange("p (m u) -> p m u", u=2),
+                banks[i][:].rearrange("p u m -> p m u"),
+            )
+
+        def quantise(i):
+            if i < PACK:
+                cols = slice(i * P, (i + 1) * P)
+                nc.vector.quantize_mx(g_codes[:, cols].bitcast(E5M2), g_scales[:, cols], grouped[i])
+                return
+            x_codes = x_codes_all[:, (i - PACK) * P : (i - PACK + 1) * P]
+            x_scales = keep.tile([P, P], U8, name="x_scales%d" % i, align_bytes=64)
+            nc.vector.quantize_mx(x_codes.bitcast(E4M3), x_scales[:], grouped[i])
+            acc = psum.tile([P, N], F32, name="acc%d" % i, tag="bank%d" % i)
             nc.tensor.matmul_mx(
                 acc[:],
-                lhsT=x_codes[:].bitcast(E4M3),
+                lhsT=x_codes.bitcast(E4M3),
                 lhsT_scale=x_scales[:],
                 rhs=g_codes[:].bitcast(E5M2),
                 rhs_scale=g_scales[:],
                 start=True,
                 stop=True,
             )
-            nc.scalar.activation(y[:, t, :], acc[:], COPY, scale=OUT_SCALE)
-            nc.sync.dma_start(y_rows[t], y[:, t, :])
+            sums_of[i - PACK] = acc
+
+        for i in range(TILES):
+            gather_and_turn(i)
+            if i >= 1:
+                regroup(i - 1)
+        y_flat = keep.tile([P, PACK * N], F32, name="y_flat", align_bytes=64)
+        y = y_flat[:].rearrange("p (t n) -> p t n", t=PACK)
+        regroup(TILES - 1, y_flat)
+        g_codes = keep.tile([P, N], U32, name="g_codes", tag="window%d" % (TILES - 1), align_bytes=64)
+        x_codes_all = keep.tile([P, K], U32, name="x_codes", tag="stage%d_1" % (TILES - 1), align_bytes=64)
+        for i in range(TILES):
+            quantise(i)
+        nc.scalar.activation(y[:, 0, :], sums_of[0][:], COPY, scale=OUT_SCALE)
+        nc.sync.dma_start(y_rows[0], y[:, 0, :])
+        nc.scalar.activation(y[:, 1, :], sums_of[1][:], COPY, scale=OUT_SCALE)
+        nc.sync.dma_start(y_rows[1], y[:, 1, :])
+        nc.vector.tensor_scalar_mul(y[:, 2, :], sums_of[2][:], OUT_SCALE)
+        nc.sync.dma_start(y_rows[2], y[:, 2, :])
+        for q in range(4):
+            cols = slice(q * N // 4, (q + 1) * N // 4)
+            nc.scalar.activation(y[:, 3, cols], sums_of[3][:, cols], COPY, scale=OUT_SCALE)
+        nc.sync.dma_start(y_rows[3], y[:, 3, :])
 
         y_grouped = keep.tile([P, N, PACK], BF16, name="y_grouped", align_bytes=64)
         y_codes = keep.tile([P, N], U32, name="y_codes", align_bytes=64)
         y_scales = keep.tile([P, N], U8, name="y_scales", align_bytes=64)
-        nc.vector.tensor_copy(
-            y_grouped[:].rearrange("p (c i) t -> p c t i", i=4),
-            y[:].rearrange("p t (c i) -> p c t i", i=4),
-        )
-        nc.vector.quantize_mx(y_codes[:].bitcast(E4M3), y_scales[:], y_grouped[:].rearrange("p n t -> p (n t)"))
-        nc.sync.dma_start(out_1[0].rearrange("p n t -> p (n t)").bitcast(I32), y_codes[:].bitcast(I32))
+        for copy, cols in (
+            (nc.vector.tensor_copy, slice(0, 128)),
+            (nc.vector.tensor_copy, slice(128, 256)),
+            (nc.vector.tensor_copy, slice(256, 384)),
+            (nc.scalar.copy, slice(384, 512)),
+        ):
+            copy(
+                y_grouped[:, cols, :].rearrange("p (c i) t -> p c t i", i=4),
+                y[:, :, cols].rearrange("p t (c i) -> p c t i", i=4),
+            )
+        word_rows = out_1[0].rearrange("p n t -> p (n t)").bitcast(I32)
+        for h in range(2):
+            cols = slice(h * N // 2, (h + 1) * N // 2)
+            nc.vector.quantize_mx(
+                y_codes[:, cols].bitcast(E4M3), y_scales[:, cols], y_grouped[:, cols, :].rearrange("p n t -> p (n t)")
+            )
+            nc.sync.dma_start(word_rows[:, cols], y_codes[:, cols].bitcast(I32))
         scale_rows = out_2[0].bitcast(I32)
         for q in range(4):
-            queue = nc.sync if q % 2 else nc.scalar
+            queue = nc.sync if q == 3 else nc.scalar
             queue.dma_start(scale_rows[4 * q : 4 * q + 4, :], y_scales[32 * q : 32 * q + 4, :].bitcast(I32))

@@ -33,16 +33,16 @@ def tile_moe_expert_heads_wgrad_pl_kernel(tc, xf, g, ra, rb, offs, offs2, out_0,
 
         x_list = keep.tile([P, J // 16], U16, name="x_list")
         g_list = keep.tile([P, J // 16], U16, name="g_list")
-        ra_col = keep.tile([P, 2, 2], F32, name="ra_col")
-        rb_col = keep.tile([P, 2, 2], F32, name="rb_col")
+        ra_col = keep.tile([P, PACK], F32, name="ra_col")
+        rb_col = keep.tile([P, PACK], F32, name="rb_col")
         windows = [keep.tile([P, T], F32, name="window%d" % i, tag="window%d" % i, align_bytes=64) for i in range(TILES)]
         x_rows = xf.rearrange("(p t) c -> t p c", t=PACK)
         g_rows = g.rearrange("(u p) c -> u p c", p=P)
 
-        nc.scalar.dma_start(rb_col[:], rb[0].rearrange("(h p c) -> p h c", h=2, c=2))
+        nc.scalar.dma_start(rb_col[:], rb[0].rearrange("(p c) -> p c", c=PACK))
         nc.sync.dma_start(g_list[:], offs2)
         nc.sync.dma_start(windows[0][:], g_rows[0])
-        nc.scalar.dma_start(ra_col[:], ra[0].rearrange("(h p c) -> p h c", h=2, c=2))
+        nc.scalar.dma_start(ra_col[:], ra[0].rearrange("(p c) -> p c", c=PACK))
         nc.sync.dma_start(windows[1][:], g_rows[1])
         nc.sync.dma_start(x_list[:], offs)
         for u in range(2, PACK):
@@ -53,28 +53,31 @@ def tile_moe_expert_heads_wgrad_pl_kernel(tc, xf, g, ra, rb, offs, offs2, out_0,
         ident = keep.tile([P, P], F32, name="ident")
         make_identity(nc, ident[:])
 
-        def spread(col, name, first_bank):
+        def spread(col, name, bank_tag):
             row = keep.tile([P, J], F32, name=name)
-            for h in range(2):
-                bank = psum.tile([P, 2, P], F32, name="%s_bank%d" % (name, h), tag="bank%d" % (first_bank + h))
-                for c in range(2):
-                    nc.tensor.transpose(bank[:, c, :], col[:, h, c : c + 1].to_broadcast([P, P]), ident[:])
-                nc.scalar.copy(
-                    row[:, h * HALF : (h + 1) * HALF].rearrange("q (p c) -> q p c", c=2),
-                    bank[:].rearrange("q c p -> q p c"),
-                )
+            bank = psum.tile([P, PACK, P], F32, name=name + "_bank", tag=bank_tag)
+            for c in range(PACK):
+                nc.tensor.transpose(bank[:, c, :], col[:, c : c + 1].to_broadcast([P, P]), ident[:])
+            nc.scalar.copy(row[:].rearrange("q (p c) -> q p c", c=PACK), bank[:].rearrange("q c p -> q p c"))
             return row
 
-        rb_row = spread(rb_col, "rb_row", 0)
-        ra_row = spread(ra_col, "ra_row", 2)
+        rb_row = spread(rb_col, "rb_row", "bank2")
+        ra_row = spread(ra_col, "ra_row", "bank3")
 
         g_scales = keep.tile([P, N], U8, name="g_scales", align_bytes=64)
         y_rows = out_0.rearrange("(p t) n -> t p n", t=PACK)
         banks, grouped, sums_of = {}, {}, {}
 
         def gather_and_turn(i):
+            if i == 0:
+                picked = keep.tile([P, J], F32, name="picked0")
+                nc.vector.tensor_copy(picked[:], windows[0][:].indirect(g_list[:]))
+                banks[0] = psum.tile([P, PACK, P], F32, name="turned0", tag="bank0")
+                for r in range(PACK):
+                    nc.tensor.transpose(banks[0][:, r, :], picked[:, r:J:PACK], ident[:])
+                return
             offsets, weights = (g_list, rb_row) if i < PACK else (x_list, ra_row)
-            pieces = 2 if i in (0, TILES - 1) else 1
+            pieces = 2 if i == TILES - 1 else 1
             width = J // pieces
             pairs = ring.tile([P, 2, P, 2], BF16, name="pairs")
             for h in range(pieces):
@@ -99,8 +102,12 @@ def tile_moe_expert_heads_wgrad_pl_kernel(tc, xf, g, ra, rb, offs, offs2, out_0,
             if i == TILES - 1:
                 grouped[i] = y_flat[:, 2 * N - P : 2 * N + P].bitcast(BF16)
             else:
-                tag = "stage%d_0" % (i + 1)
+                tag = "window%d" % (i + 1)
                 grouped[i] = keep.tile([P, J], BF16, name="grouped%d" % i, tag=tag, align_bytes=64)[:]
+            if i == 0:
+                for r in range(PACK):
+                    nc.scalar.activation(grouped[0][:, r:J:PACK], banks[0][:, r, :], COPY, scale=rb_col[:, r : r + 1])
+                return
             nc.scalar.copy(
                 grouped[i].bitcast(F32).rearrange("p (m u) -> p m u", u=2),
                 banks[i][:].rearrange("p u m -> p m u"),
@@ -133,7 +140,7 @@ def tile_moe_expert_heads_wgrad_pl_kernel(tc, xf, g, ra, rb, offs, offs2, out_0,
         y_flat = keep.tile([P, PACK * N], F32, name="y_flat", align_bytes=64)
         y = y_flat[:].rearrange("p (t n) -> p t n", t=PACK)
         regroup(TILES - 1, y_flat)
-        g_codes = keep.tile([P, N], U32, name="g_codes", tag="window%d" % (TILES - 1), align_bytes=64)
+        g_codes = keep.tile([P, N], U32, name="g_codes", tag="stage%d_0" % (TILES - 1), align_bytes=64)
         x_codes_all = keep.tile([P, K], U32, name="x_codes", tag="stage%d_1" % (TILES - 1), align_bytes=64)
         for i in range(TILES):
             quantise(i)

from contextlib import ExitStack

import concourse.mybir as mybir
from concourse.masks import make_identity

K, N, T, J = 512, 512, 1024, 512
FLOPS = 2 * K * N * J

F32 = mybir.dt.float32
BF16 = mybir.dt.bfloat16
I32 = mybir.dt.int32
U32 = mybir.dt.uint32
U16 = mybir.dt.uint16
U8 = mybir.dt.uint8
E4M3 = mybir.dt.float8_e4m3fn_x4
E5M2 = mybir.dt.float8_e5m2_x4
MULT = mybir.AluOpType.mult
COPY = mybir.ActivationFunctionType.Copy

P = 128
PACK = 4
TILES = 2 * PACK
HALF = J // 2
OUT_SCALE = 0.04


def tile_moe_expert_heads_wgrad_pl_kernel(tc, xf, g, ra, rb, offs, offs2, out_0, out_1, out_2):
    nc = tc.nc
    with ExitStack() as ctx:
        keep = ctx.enter_context(tc.tile_pool(name="keep", bufs=1))
        ring = ctx.enter_context(tc.tile_pool(name="ring", bufs=3))
        psum = ctx.enter_context(tc.psum_pool(name="psum", bufs=1))

        x_list = keep.tile([P, J // 16], U16, name="x_list")
        g_list = keep.tile([P, J // 16], U16, name="g_list")
        ra_col = keep.tile([P, PACK], F32, name="ra_col")
        rb_col = keep.tile([P, PACK], F32, name="rb_col")
        windows = [keep.tile([P, T], F32, name="window%d" % i, tag="window%d" % i, align_bytes=64) for i in range(TILES)]
        x_rows = xf.rearrange("(p t) c -> t p c", t=PACK)
        g_rows = g.rearrange("(u p) c -> u p c", p=P)

        nc.scalar.dma_start(rb_col[:], rb[0].rearrange("(p c) -> p c", c=PACK))
        nc.sync.dma_start(g_list[:], offs2)
        nc.sync.dma_start(windows[0][:], g_rows[0])
        nc.scalar.dma_start(ra_col[:], ra[0].rearrange("(p c) -> p c", c=PACK))
        nc.sync.dma_start(windows[1][:], g_rows[1])
        nc.sync.dma_start(x_list[:], offs)
        for u in range(2, PACK):
            nc.sync.dma_start(windows[u][:], g_rows[u])
        for t in range(PACK):
            nc.sync.dma_start(windows[PACK + t][:], x_rows[t])

        ident = keep.tile([P, P], F32, name="ident")
        make_identity(nc, ident[:])

        def spread(col, name, bank_tag):
            row = keep.tile([P, J], F32, name=name)
            bank = psum.tile([P, PACK, P], F32, name=name + "_bank", tag=bank_tag)
            for c in range(PACK):
                nc.tensor.transpose(bank[:, c, :], col[:, c : c + 1].to_broadcast([P, P]), ident[:])
            nc.scalar.copy(row[:].rearrange("q (p c) -> q p c", c=PACK), bank[:].rearrange("q c p -> q p c"))
            return row

        rb_row = spread(rb_col, "rb_row", "bank2")
        ra_row = spread(ra_col, "ra_row", "bank3")

        g_scales = keep.tile([P, N], U8, name="g_scales", align_bytes=64)
        y_rows = out_0.rearrange("(p t) n -> t p n", t=PACK)
        banks, grouped, sums_of = {}, {}, {}

        def gather_and_turn(i):
            if i == 0:
                picked = keep.tile([P, J], F32, name="picked0")
                nc.vector.tensor_copy(picked[:], windows[0][:].indirect(g_list[:]))
                banks[0] = psum.tile([P, PACK, P], F32, name="turned0", tag="bank0")
                for r in range(PACK):
                    nc.tensor.transpose(banks[0][:, r, :], picked[:, r:J:PACK], ident[:])
                return
            offsets, weights = (g_list, rb_row) if i < PACK else (x_list, ra_row)
            pieces = 2 if i == TILES - 1 else 1
            width = J // pieces
            pairs = ring.tile([P, 2, P, 2], BF16, name="pairs")
            for h in range(pieces):
                slots = slice(h * width, (h + 1) * width)
                picked = keep.tile([P, width], F32, name="picked%d_%d" % (i, h), tag="stage%d_%d" % (i, h), align_bytes=64)
                nc.vector.tensor_tensor(
                    picked[:],
                    windows[i][:].indirect(offsets[:, h * width // 16 : (h + 1) * width // 16]),
                    weights[:, slots],
                    MULT,
                )
                nc.scalar.copy(
                    pairs[:, :, h * width // PACK : (h + 1) * width // PACK, :],
                    picked[:].rearrange("q (p u e) -> q u p e", u=2, e=2),
                )
            words = pairs[:].rearrange("q u p e -> q (u p e)").bitcast(F32)
            banks[i] = psum.tile([P, 2, P], F32, name="turned%d" % i, tag="bank%d" % (i % 4))
            for u in range(2):
                nc.tensor.transpose(banks[i][:, u, :], words[:, u * P : (u + 1) * P], ident[:])

        def regroup(i, y_flat=None):
            if i == TILES - 1:
                grouped[i] = y_flat[:, 2 * N - P : 2 * N + P].bitcast(BF16)
            else:
                tag = "window%d" % (i + 1)
                grouped[i] = keep.tile([P, J], BF16, name="grouped%d" % i, tag=tag, align_bytes=64)[:]
            if i == 0:
                for r in range(PACK):
                    nc.scalar.activation(grouped[0][:, r:J:PACK], banks[0][:, r, :], COPY, scale=rb_col[:, r : r + 1])
                return
            nc.scalar.copy(
                grouped[i].bitcast(F32).rearrange("p (m u) -> p m u", u=2),
                banks[i][:].rearrange("p u m -> p m u"),
            )

        def quantise(i):
            if i < PACK:
                cols = slice(i * P, (i + 1) * P)
                nc.vector.quantize_mx(g_codes[:, cols].bitcast(E5M2), g_scales[:, cols], grouped[i])
                return
            x_codes = x_codes_all[:, (i - PACK) * P : (i - PACK + 1) * P]
            x_scales = keep.tile([P, P], U8, name="x_scales%d" % i, align_bytes=64)
            nc.vector.quantize_mx(x_codes.bitcast(E4M3), x_scales[:], grouped[i])
            acc = psum.tile([P, N], F32, name="acc%d" % i, tag="bank%d" % i)
            nc.tensor.matmul_mx(
                acc[:],
                lhsT=x_codes.bitcast(E4M3),
                lhsT_scale=x_scales[:],
                rhs=g_codes[:].bitcast(E5M2),
                rhs_scale=g_scales[:],
                start=True,
                stop=True,
            )
            sums_of[i - PACK] = acc

        for i in range(TILES):
            gather_and_turn(i)
            if i >= 1:
                regroup(i - 1)
        y_flat = keep.tile([P, PACK * N], F32, name="y_flat", align_bytes=64)
        y = y_flat[:].rearrange("p (t n) -> p t n", t=PACK)
        regroup(TILES - 1, y_flat)
        g_codes = keep.tile([P, N], U32, name="g_codes", tag="stage%d_0" % (TILES - 1), align_bytes=64)
        x_codes_all = keep.tile([P, K], U32, name="x_codes", tag="stage%d_1" % (TILES - 1), align_bytes=64)
        for i in range(TILES):
            quantise(i)
        nc.scalar.activation(y[:, 0, :], sums_of[0][:], COPY, scale=OUT_SCALE)
        nc.sync.dma_start(y_rows[0], y[:, 0, :])
        nc.scalar.activation(y[:, 1, :], sums_of[1][:], COPY, scale=OUT_SCALE)
        nc.sync.dma_start(y_rows[1], y[:, 1, :])
        nc.vector.tensor_scalar_mul(y[:, 2, :], sums_of[2][:], OUT_SCALE)
        nc.sync.dma_start(y_rows[2], y[:, 2, :])
        for q in range(4):
            cols = slice(q * N // 4, (q + 1) * N // 4)
            nc.scalar.activation(y[:, 3, cols], sums_of[3][:, cols], COPY, scale=OUT_SCALE)
        nc.sync.dma_start(y_rows[3], y[:, 3, :])

        y_grouped = keep.tile([P, N, PACK], BF16, name="y_grouped", align_bytes=64)
        y_codes = keep.tile([P, N], U32, name="y_codes", align_bytes=64)
        y_scales = keep.tile([P, N], U8, name="y_scales", align_bytes=64)
        for copy, cols in (
            (nc.vector.tensor_copy, slice(0, 128)),
            (nc.vector.tensor_copy, slice(128, 256)),
            (nc.vector.tensor_copy, slice(256, 384)),
            (nc.scalar.copy, slice(384, 512)),
        ):
            copy(
                y_grouped[:, cols, :].rearrange("p (c i) t -> p c t i", i=4),
                y[:, :, cols].rearrange("p t (c i) -> p c t i", i=4),
            )
        word_rows = out_1[0].rearrange("p n t -> p (n t)").bitcast(I32)
        for h in range(2):
            cols = slice(h * N // 2, (h + 1) * N // 2)
            nc.vector.quantize_mx(
                y_codes[:, cols].bitcast(E4M3), y_scales[:, cols], y_grouped[:, cols, :].rearrange("p n t -> p (n t)")
            )
            nc.sync.dma_start(word_rows[:, cols], y_codes[:, cols].bitcast(I32))
        scale_rows = out_2[0].bitcast(I32)
        for q in range(4):
            queue = nc.sync if q == 3 else nc.scalar
            queue.dma_start(scale_rows[4 * q : 4 * q + 4, :], y_scales[32 * q : 32 * q + 4, :].bitcast(I32))
